import numpy as np
import ml_dtypes


def mxq(x, axis, fmt="e4m3"):
    dtype, down = {"e4m3": (ml_dtypes.float8_e4m3fn, 7), "e5m2": (ml_dtypes.float8_e5m2, 14)}[fmt]
    v = np.moveaxis(np.asarray(x, np.float32).astype(ml_dtypes.bfloat16).astype(np.float64), axis, -1)
    blocks = v.reshape(v.shape[:-1] + (-1, 32))
    amax = np.abs(blocks).max(-1, keepdims=True)
    byte = np.maximum(np.where(amax > 0, np.frexp(amax)[1] - 1 + 127, 0) - down, 1)
    scale = np.exp2(byte - 127.0)
    codes = (blocks / scale).astype(np.float32).astype(dtype).astype(np.float64)
    return np.moveaxis((codes * scale).reshape(v.shape), -1, axis)


WIDE = False


def mx_kscale(k):
    if not WIDE:
        return np.ones(k)
    levels = np.array([30, -30])
    if k % 512:
        return np.exp2(np.random.permutation(np.resize(levels, k // 32))).repeat(32)
    a = np.empty((k // 512, 16))
    for p in range(k // 512):
        a[p, :8] = np.random.permutation(np.resize(levels, 8))
        for g in range(8):
            far = levels[np.abs(levels - a[p, g]) >= 10]
            a[p, g + 8] = far[np.random.randint(len(far))]
    return np.exp2(a.ravel()).repeat(32)


def f64(x):
    return np.asarray(x).astype(np.float64)


def striped(idx):
    return np.tile(np.asarray(idx).reshape(-1, 16).T, (8, 1)).astype(np.uint16)


def unstriped(offs):
    return offs[:16].T.reshape(-1).astype(np.int64)


E2M1 = np.array([0.0, 0.5, 1.0, 1.5, 2.0, 3.0, 4.0, 6.0, -0.0, -0.5, -1.0, -1.5, -2.0, -3.0, -4.0, -6.0])


def pack_weight(w, fmt):
    k, n = w.shape
    w = f64(np.asarray(w, np.float32).astype(ml_dtypes.bfloat16)).reshape(k // 32, 32, n)
    amax = np.abs(w).max(1)
    if fmt in ("e4m3", "e5m2"):
        byte = np.frexp(amax)[1] - 1 + 127 - (7 if fmt == "e4m3" else 14)
    else:
        mant, ex = np.frexp(amax / 6.0)
        byte = np.where(mant > 0.5, ex, ex - 1) + 127
    byte = np.clip(np.where(amax > 0, byte, 1), 1, 254)
    scaled = (w * np.exp2(127.0 - byte)[:, None, :]).reshape(k, n).astype(np.float32)
    by_word = np.ascontiguousarray(scaled.reshape(k // 512, 128, 4, n).transpose(0, 1, 3, 2))
    if fmt in ("e4m3", "e5m2"):
        words = by_word.astype(ml_dtypes.float8_e4m3fn if fmt == "e4m3" else ml_dtypes.float8_e5m2).view(np.uint8)
    else:
        c = by_word.astype(ml_dtypes.float4_e2m1fn).view(np.uint8) & 0xF
        words = (c[..., 0::2] | (c[..., 1::2] << 4)).reshape(k // 512, 128, 2 * n)
    return np.ascontiguousarray(words), np.ascontiguousarray(byte.astype(np.uint8).reshape(k // 512, 16, n))


def unpack_weight(words, scales, fmt):
    g, _, n = scales.shape
    words = np.ascontiguousarray(words).reshape(g, 128, n, -1)
    if fmt in ("e4m3", "e5m2"):
        vals = words.view(ml_dtypes.float8_e4m3fn if fmt == "e4m3" else ml_dtypes.float8_e5m2).astype(np.float64)
    else:
        nib = np.empty((g, 128, n, 4), np.uint8)
        nib[..., 0::2] = words & 0xF
        nib[..., 1::2] = words >> 4
        vals = E2M1[nib]
    vals = vals * np.repeat(np.exp2(scales.astype(np.float64) - 127.0), 8, axis=1)[..., None]
    return vals.transpose(0, 1, 3, 2).reshape(g * 512, n)


K, T, J, R, C, O, N = 512, 1024, 256, 512, 512, 128, 256


def setup_inputs():
    n = np.random.standard_normal
    idx = np.random.permutation(T)[:J]
    idx2 = np.random.permutation(C)[:J]
    idx3 = np.random.permutation(C)[:O]
    idx4 = np.random.permutation(J)[:O]
    idx5 = np.random.permutation(T)[:O]
    fk = mx_kscale(K)
    fr = mx_kscale(R)
    xtp = pack_weight(n((K, T)) / fk[:, None], "e4m3")
    wp = pack_weight(n((K, R)) * 1 / np.sqrt(K) * fk[:, None] * fr, "e2m1")
    w2p = pack_weight(n((K, R)) * 1 / np.sqrt(K) * fk[:, None] * fr, "e5m2")
    wbp = pack_weight(n((R, N)) * 1 / np.sqrt(R) / fr[:, None], "e5m2")
    wsp = pack_weight(n((K, N)) * 1 / np.sqrt(K) * fk[:, None], "e5m2")
    return {
        "xt_words": xtp[0],
        "xt_scales": xtp[1],
        "w_words": wp[0],
        "w_scales": wp[1],
        "w2_words": w2p[0],
        "w2_scales": w2p[1],
        "wb_words": wbp[0],
        "wb_scales": wbp[1],
        "ws_words": wsp[0],
        "ws_scales": wsp[1],
        "offs": striped(idx),
        "offs2": striped(idx2),
        "offs3": striped(idx3),
        "offs4": striped(idx4),
        "offs5": striped(idx5),
    }


def reference(xt_words, xt_scales, w_words, w_scales, w2_words, w2_scales, wb_words, wb_scales, ws_words, ws_scales, offs, offs2, offs3, offs4, offs5):
    idx = unstriped(offs)
    idx2 = unstriped(offs2)
    idx3 = unstriped(offs3)
    idx4 = unstriped(offs4)
    idx5 = unstriped(offs5)
    xtu = unpack_weight(xt_words, xt_scales, "e4m3")
    wu = unpack_weight(w_words, w_scales, "e2m1")
    w2u = unpack_weight(w2_words, w2_scales, "e5m2")
    wbu = unpack_weight(wb_words, wb_scales, "e5m2")
    wsu = unpack_weight(ws_words, ws_scales, "e5m2")
    xtidxg = xtu[:, idx]
    a = wu.T @ xtidxg
    b = w2u.T @ xtidxg
    pw = np.zeros((R, C))
    pw[:, idx2] = a
    hid = np.maximum(pw[:, idx3], b[:, idx4])
    hidq = mxq(hid, 0, "e4m3")
    xtidx5g = xtu[:, idx5]
    y = wbu.T @ hidq + wsu.T @ xtidx5g
    return y

@@ -1,0 +1,175 @@
+from contextlib import ExitStack
+
+import concourse.mybir as mybir
+
+K, T, J, R, C, O, N = 512, 1024, 256, 512, 512, 128, 256
+FLOPS = 2 * (2 * K * R * J + R * N * O + K * N * O)
+
+F32 = mybir.dt.float32
+BF16 = mybir.dt.bfloat16
+I32 = mybir.dt.int32
+U32 = mybir.dt.uint32
+U16 = mybir.dt.uint16
+U8 = mybir.dt.uint8
+E4M3 = mybir.dt.float8_e4m3fn_x4
+E5M2 = mybir.dt.float8_e5m2_x4
+E2M1 = mybir.dt.float4_e2m1fn_x4
+COPY = mybir.ActivationFunctionType.Copy
+MAX = mybir.AluOpType.max
+
+P = 128
+PACK = 4
+
+
+def load_words(queue, tile, words):
+    queue.dma_start(out=tile[:].bitcast(I32), in_=words.bitcast(I32))
+
+
+def load_scale_rows(queue, tile, scales, q):
+    queue.dma_start(out=tile[32 * q : 32 * q + 4, :].bitcast(I32), in_=scales[0, 4 * q : 4 * q + 4, :].bitcast(I32))
+
+
+def tile_list_postbox_twow_further_plain_kernel(
+    tc, xt_words, xt_scales, w_words, w_scales, w2_words, w2_scales, wb_words, wb_scales,
+    ws_words, ws_scales, offs, offs2, offs3, offs4, offs5, out,
+):
+    nc = tc.nc
+    with ExitStack() as ctx:
+        pool = ctx.enter_context(tc.tile_pool(name="held", bufs=1))
+        psum = ctx.enter_context(tc.psum_pool(name="psum", bufs=1))
+
+        def sbuf(name, shape, dtype):
+            return pool.tile(shape, dtype, name=name, align_bytes=64)
+
+        def flat(words):
+            return words[0].rearrange("p n t -> p (n t)")
+
+        def load_list(name, src):
+            tile = pool.tile(list(src.shape), U16, name=name)
+            nc.sync.dma_start(tile[:], src)
+            return tile
+
+        xt_w = sbuf("xt_w", [P, T], U32)
+        xt_s = sbuf("xt_s", [P, T], U8)
+        w_raw = sbuf("w_raw", [P, R], U16)
+        w_sraw = sbuf("w_sraw", [P, R], U8)
+        w2_raw = sbuf("w2_raw", [P, R], U32)
+        w2_sraw = sbuf("w2_sraw", [P, R], U8)
+        wb_w = sbuf("wb_w", [P, N], U32)
+        wb_s = sbuf("wb_s", [P, N], U8)
+        ws_w = sbuf("ws_w", [P, N], U32)
+        ws_s = sbuf("ws_s", [P, N], U8)
+
+        for plane in (xt_s, w_sraw):
+            nc.vector.memset(plane[:].bitcast(I32), 0)
+        for plane in (w2_sraw, ws_s, wb_s):
+            nc.gpsimd.memset(plane[:].bitcast(I32), 0)
+
+        idx = load_list("idx", offs)
+        load_words(nc.sync, w_raw, w_words[0])
+        load_scale_rows(nc.sync, xt_s, xt_scales, 0)
+        load_words(nc.sync, xt_w, flat(xt_words))
+        for q in range(1, 4):
+            load_scale_rows(nc.sync, xt_s, xt_scales, q)
+        for q in range(4):
+            load_scale_rows(nc.sync, w_sraw, w_scales, q)
+        idx2 = load_list("idx2", offs2)
+        idx5 = load_list("idx5", offs5)
+        load_words(nc.sync, w2_raw, flat(w2_words))
+        for q in range(4):
+            load_scale_rows(nc.sync, w2_sraw, w2_scales, q)
+        idx3 = load_list("idx3", offs3)
+        idx4 = load_list("idx4", offs4)
+        load_words(nc.sync, ws_w, flat(ws_words))
+        for q in range(4):
+            load_scale_rows(nc.sync, ws_s, ws_scales, q)
+        load_words(nc.sync, wb_w, flat(wb_words))
+        for q in range(4):
+            load_scale_rows(nc.sync, wb_s, wb_scales, q)
+
+        boards = [sbuf("board%d" % t, [P, C], F32) for t in range(PACK)]
+        for t in range(PACK):
+            nc.vector.memset(boards[t][:], 0.0)
+
+        w_w = sbuf("w_w", [P, R], U16)
+        w_s = sbuf("w_s", [P, R], U8)
+        w2_w = sbuf("w2_w", [P, R], U32)
+        w2_s = sbuf("w2_s", [P, R], U8)
+        nc.vector.tensor_copy(
+            out=w_w[:].rearrange("p (t m) -> p t m", t=PACK), in_=w_raw[:].rearrange("p (m t) -> p t m", t=PACK))
+        nc.gpsimd.tensor_copy(
+            out=w2_w[:].rearrange("p (t c i) -> p c t i", t=PACK, i=4),
+            in_=w2_raw[:].rearrange("p (c i t) -> p c t i", t=PACK, i=4))
+        nc.gpsimd.tensor_copy(
+            out=w2_s[:].rearrange("p (t m) -> p t m", t=PACK), in_=w2_sraw[:].rearrange("p (m t) -> p t m", t=PACK))
+
+        xg_w = sbuf("xg_w", [P, J], U32)
+        xg_s = sbuf("xg_s", [P, J], U8)
+        x5_w = sbuf("x5_w", [P, O], U32)
+        x5_s = sbuf("x5_s", [P, O], U8)
+        nc.vector.tensor_copy(out=xg_s[:], in_=xt_s[:].indirect(idx[:]))
+        nc.vector.tensor_copy(out=xg_w[:], in_=xt_w[:].indirect(idx[:]))
+        nc.vector.tensor_copy(
+            out=w_s[:].rearrange("p (t m) -> p t m", t=PACK), in_=w_sraw[:].rearrange("p (m t) -> p t m", t=PACK))
+        nc.vector.tensor_copy(out=x5_s[:], in_=xt_s[:].indirect(idx5[:]))
+        nc.vector.tensor_copy(out=x5_w[:], in_=xt_w[:].indirect(idx5[:]))
+
+        def first_stage(acc, words, scales, fmt, t):
+            cols = slice(t * P, (t + 1) * P)
+            nc.tensor.matmul_mx(out=acc, lhsT=words[:, cols].bitcast(fmt), lhsT_scale=scales[:, cols],
+                                rhs=xg_w[:].bitcast(E4M3), rhs_scale=xg_s[:], start=True, stop=True)
+
+        a_ps = [psum.tile([P, J], F32, name="a_ps%d" % t) for t in range(PACK)]
+        b_ps = [psum.tile([P, 2, J], F32, name="b_ps%d" % u) for u in range(2)]
+        y_ps = [psum.tile([P, O], F32, name="y_ps%d" % h) for h in range(2)]
+        for t in range(PACK):
+            first_stage(a_ps[t][:], w_w, w_s, E2M1, t)
+        for t in range(PACK):
+            first_stage(b_ps[t // 2][:, t % 2, :], w2_w, w2_s, E5M2, t)
+        for h in range(2):
+            cols = slice(h * P, (h + 1) * P)
+            nc.tensor.matmul_mx(out=y_ps[h][:], lhsT=ws_w[:, cols].bitcast(E5M2), lhsT_scale=ws_s[:, cols],
+                                rhs=x5_w[:].bitcast(E4M3), rhs_scale=x5_s[:], start=True, stop=False)
+
+        def move(on_scalar, dst, src):
+            if on_scalar:
+                nc.scalar.activation(out=dst, in_=src, func=COPY)
+            else:
+                nc.vector.tensor_copy(out=dst, in_=src)
+
+        a_sb = [sbuf("a_sb%d" % t, [P, J], F32) for t in range(PACK)]
+        b_sb = [sbuf("b_sb%d" % u, [P, 2 * J], F32) for u in range(2)]
+        from_board = sbuf("from_board", [P, PACK, O], F32)
+        from_b = sbuf("from_b", [P, PACK, O], F32)
+        for t in range(PACK):
+            move(t % 2 == 0, a_sb[t][:], a_ps[t][:])
+        for t in range(2):
+            move(t % 2 == 0, boards[t][:].indirect(idx2[:]), a_sb[t][:])
+        for u in range(2):
+            move(True, b_sb[u][:], b_ps[u][:].rearrange("p t j -> p (t j)"))
+        for t in range(2):
+            move(t % 2 == 0, from_board[:, t, :], boards[t][:].indirect(idx3[:]))
+        for t in range(PACK):
+            window = b_sb[t // 2][:, (t % 2) * J : (t % 2 + 1) * J]
+            move(t == 0, from_b[:, t, :], window.indirect(idx4[:]))
+        for t in range(2, PACK):
+            move(t % 2 == 0, boards[t][:].indirect(idx2[:]), a_sb[t][:])
+        for t in range(2, PACK):
+            move(t % 2 == 0, from_board[:, t, :], boards[t][:].indirect(idx3[:]))
+
+        hid = sbuf("hid", [P, O * PACK], BF16)
+        nc.vector.tensor_tensor(
+            out=hid[:].rearrange("p (c i t) -> p c t i", t=PACK, i=4),
+            in0=from_board[:].rearrange("p t (c i) -> p c t i", i=4),
+            in1=from_b[:].rearrange("p t (c i) -> p c t i", i=4), op=MAX)
+        hid_w = sbuf("hid_w", [P, O], U32)
+        hid_s = sbuf("hid_s", [P, O], U8)
+        nc.vector.quantize_mx(out=hid_w[:].bitcast(E4M3), scales=hid_s[:], in_=hid[:])
+
+        for h in range(2):
+            cols = slice(h * P, (h + 1) * P)
+            nc.tensor.matmul_mx(out=y_ps[h][:], lhsT=wb_w[:, cols].bitcast(E5M2), lhsT_scale=wb_s[:, cols],
+                                rhs=hid_w[:].bitcast(E4M3), rhs_scale=hid_s[:], start=False, stop=True)
+            y_sb = sbuf("y_sb%d" % h, [P, O], F32)
+            move(h == 1, y_sb[:], y_ps[h][:])
+            (nc.scalar if h == 1 else nc.sync).dma_start(out=out[cols, :], in_=y_sb[:])

@@ -29,6 +29,12 @@ def load_scale_rows(queue, tile, scales, q):
     queue.dma_start(out=tile[32 * q : 32 * q + 4, :].bitcast(I32), in_=scales[0, 4 * q : 4 * q + 4, :].bitcast(I32))
 
 
+def load_scale_quadrant(queue, tile, scales, q):
+    rows = scales[0, 4 * q : 4 * q + 4, :].bitcast(I32)
+    queue.dma_start(out=tile[32 * q : 32 * q + 32, :].bitcast(I32),
+                    in_=rows.unsqueeze(0).broadcast_to([8, 4, rows.shape[1]]))
+
+
 def tile_list_postbox_twow_further_plain_kernel(
     tc, xt_words, xt_scales, w_words, w_scales, w2_words, w2_scales, wb_words, wb_scales,
     ws_words, ws_scales, offs, offs2, offs3, offs4, offs5, out,
@@ -60,21 +66,19 @@ def tile_list_postbox_twow_further_plain_kernel(
         ws_w = sbuf("ws_w", [P, N], U32)
         ws_s = sbuf("ws_s", [P, N], U8)
 
-        for plane in (xt_s, w_sraw):
-            nc.vector.memset(plane[:].bitcast(I32), 0)
+        nc.vector.memset(w_sraw[:].bitcast(I32), 0)
         for plane in (w2_sraw, ws_s, wb_s):
             nc.gpsimd.memset(plane[:].bitcast(I32), 0)
 
         idx = load_list("idx", offs)
+        for q in range(4):
+            load_scale_quadrant(nc.sync, xt_s, xt_scales, q)
         load_words(nc.sync, w_raw, w_words[0])
-        load_scale_rows(nc.sync, xt_s, xt_scales, 0)
         load_words(nc.sync, xt_w, flat(xt_words))
-        for q in range(1, 4):
-            load_scale_rows(nc.sync, xt_s, xt_scales, q)
         for q in range(4):
             load_scale_rows(nc.sync, w_sraw, w_scales, q)
-        idx2 = load_list("idx2", offs2)
         idx5 = load_list("idx5", offs5)
+        idx2 = load_list("idx2", offs2)
         load_words(nc.sync, w2_raw, flat(w2_words))
         for q in range(4):
             load_scale_rows(nc.sync, w2_sraw, w2_scales, q)
@@ -95,8 +99,6 @@ def tile_list_postbox_twow_further_plain_kernel(
         w_s = sbuf("w_s", [P, R], U8)
         w2_w = sbuf("w2_w", [P, R], U32)
         w2_s = sbuf("w2_s", [P, R], U8)
-        nc.vector.tensor_copy(
-            out=w_w[:].rearrange("p (t m) -> p t m", t=PACK), in_=w_raw[:].rearrange("p (m t) -> p t m", t=PACK))
         nc.gpsimd.tensor_copy(
             out=w2_w[:].rearrange("p (t c i) -> p c t i", t=PACK, i=4),
             in_=w2_raw[:].rearrange("p (c i t) -> p c t i", t=PACK, i=4))
@@ -108,9 +110,14 @@ def tile_list_postbox_twow_further_plain_kernel(
         x5_w = sbuf("x5_w", [P, O], U32)
         x5_s = sbuf("x5_s", [P, O], U8)
         nc.vector.tensor_copy(out=xg_s[:], in_=xt_s[:].indirect(idx[:]))
-        nc.vector.tensor_copy(out=xg_w[:], in_=xt_w[:].indirect(idx[:]))
         nc.vector.tensor_copy(
-            out=w_s[:].rearrange("p (t m) -> p t m", t=PACK), in_=w_sraw[:].rearrange("p (m t) -> p t m", t=PACK))
+            out=w_w[:].rearrange("p (t m) -> p t m", t=PACK), in_=w_raw[:].rearrange("p (m t) -> p t m", t=PACK))
+        nc.vector.tensor_copy(out=xg_w[:], in_=xt_w[:].indirect(idx[:]))
+        for u in range(2):
+            pair = slice(2 * u, 2 * u + 2)
+            nc.vector.tensor_copy(
+                out=w_s[:].rearrange("p (t m) -> p t m", t=PACK)[:, pair, :],
+                in_=w_sraw[:].rearrange("p (m t) -> p t m", t=PACK)[:, pair, :])
         nc.vector.tensor_copy(out=x5_s[:], in_=xt_s[:].indirect(idx5[:]))
         nc.vector.tensor_copy(out=x5_w[:], in_=xt_w[:].indirect(idx5[:]))
 
@@ -143,25 +150,23 @@ def tile_list_postbox_twow_further_plain_kernel(
         from_b = sbuf("from_b", [P, PACK, O], F32)
         for t in range(PACK):
             move(t % 2 == 0, a_sb[t][:], a_ps[t][:])
-        for t in range(2):
+        for t in range(PACK):
             move(t % 2 == 0, boards[t][:].indirect(idx2[:]), a_sb[t][:])
-        for u in range(2):
-            move(True, b_sb[u][:], b_ps[u][:].rearrange("p t j -> p (t j)"))
-        for t in range(2):
+        for t in range(PACK):
             move(t % 2 == 0, from_board[:, t, :], boards[t][:].indirect(idx3[:]))
+        for u in range(2):
+            move(u == 0, b_sb[u][:], b_ps[u][:].rearrange("p t j -> p (t j)"))
         for t in range(PACK):
             window = b_sb[t // 2][:, (t % 2) * J : (t % 2 + 1) * J]
-            move(t == 0, from_b[:, t, :], window.indirect(idx4[:]))
-        for t in range(2, PACK):
-            move(t % 2 == 0, boards[t][:].indirect(idx2[:]), a_sb[t][:])
-        for t in range(2, PACK):
-            move(t % 2 == 0, from_board[:, t, :], boards[t][:].indirect(idx3[:]))
+            move(t != 1, from_b[:, t, :], window.indirect(idx4[:]))
 
         hid = sbuf("hid", [P, O * PACK], BF16)
-        nc.vector.tensor_tensor(
-            out=hid[:].rearrange("p (c i t) -> p c t i", t=PACK, i=4),
-            in0=from_board[:].rearrange("p t (c i) -> p c t i", i=4),
-            in1=from_b[:].rearrange("p t (c i) -> p c t i", i=4), op=MAX)
+        for u in range(2):
+            pair = slice(2 * u, 2 * u + 2)
+            nc.vector.tensor_tensor(
+                out=hid[:].rearrange("p (o t) -> p o t", t=PACK)[:, :, pair],
+                in0=from_board[:, pair, :].rearrange("p t o -> p o t"),
+                in1=from_b[:, pair, :].rearrange("p t o -> p o t"), op=MAX)
         hid_w = sbuf("hid_w", [P, O], U32)
         hid_s = sbuf("hid_s", [P, O], U8)
         nc.vector.quantize_mx(out=hid_w[:].bitcast(E4M3), scales=hid_s[:], in_=hid[:])

@@ -73,8 +73,8 @@ def tile_list_postbox_twow_further_plain_kernel(
         idx = load_list("idx", offs)
         for q in range(4):
             load_scale_quadrant(nc.sync, xt_s, xt_scales, q)
-        load_words(nc.sync, w_raw, w_words[0])
         load_words(nc.sync, xt_w, flat(xt_words))
+        load_words(nc.sync, w_raw, w_words[0])
         for q in range(4):
             load_scale_rows(nc.sync, w_sraw, w_scales, q)
         idx5 = load_list("idx5", offs5)
@@ -110,14 +110,12 @@ def tile_list_postbox_twow_further_plain_kernel(
         x5_w = sbuf("x5_w", [P, O], U32)
         x5_s = sbuf("x5_s", [P, O], U8)
         nc.vector.tensor_copy(out=xg_s[:], in_=xt_s[:].indirect(idx[:]))
-        nc.vector.tensor_copy(
+        nc.scalar.copy(
             out=w_w[:].rearrange("p (t m) -> p t m", t=PACK), in_=w_raw[:].rearrange("p (m t) -> p t m", t=PACK))
         nc.vector.tensor_copy(out=xg_w[:], in_=xt_w[:].indirect(idx[:]))
-        for u in range(2):
-            pair = slice(2 * u, 2 * u + 2)
+        for t in range(PACK):
             nc.vector.tensor_copy(
-                out=w_s[:].rearrange("p (t m) -> p t m", t=PACK)[:, pair, :],
-                in_=w_sraw[:].rearrange("p (m t) -> p t m", t=PACK)[:, pair, :])
+                out=w_s[:, t * P : (t + 1) * P], in_=w_sraw[:].rearrange("p (m t) -> p t m", t=PACK)[:, t, :])
         nc.vector.tensor_copy(out=x5_s[:], in_=xt_s[:].indirect(idx5[:]))
         nc.vector.tensor_copy(out=x5_w[:], in_=xt_w[:].indirect(idx5[:]))
 
@@ -152,10 +150,10 @@ def tile_list_postbox_twow_further_plain_kernel(
             move(t % 2 == 0, a_sb[t][:], a_ps[t][:])
         for t in range(PACK):
             move(t % 2 == 0, boards[t][:].indirect(idx2[:]), a_sb[t][:])
-        for t in range(PACK):
-            move(t % 2 == 0, from_board[:, t, :], boards[t][:].indirect(idx3[:]))
         for u in range(2):
             move(u == 0, b_sb[u][:], b_ps[u][:].rearrange("p t j -> p (t j)"))
+        for t in range(PACK):
+            move(t % 2 == 0, from_board[:, t, :], boards[t][:].indirect(idx3[:]))
         for t in range(PACK):
             window = b_sb[t // 2][:, (t % 2) * J : (t % 2 + 1) * J]
             move(t != 1, from_b[:, t, :], window.indirect(idx4[:]))
@@ -164,9 +162,9 @@ def tile_list_postbox_twow_further_plain_kernel(
         for u in range(2):
             pair = slice(2 * u, 2 * u + 2)
             nc.vector.tensor_tensor(
-                out=hid[:].rearrange("p (o t) -> p o t", t=PACK)[:, :, pair],
-                in0=from_board[:, pair, :].rearrange("p t o -> p o t"),
-                in1=from_b[:, pair, :].rearrange("p t o -> p o t"), op=MAX)
+                out=hid[:].rearrange("p (c i t) -> p c t i", t=PACK, i=4)[:, :, pair, :],
+                in0=from_board[:, pair, :].rearrange("p t (c i) -> p c t i", i=4),
+                in1=from_b[:, pair, :].rearrange("p t (c i) -> p c t i", i=4), op=MAX)
         hid_w = sbuf("hid_w", [P, O], U32)
         hid_s = sbuf("hid_s", [P, O], U8)
         nc.vector.quantize_mx(out=hid_w[:].bitcast(E4M3), scales=hid_s[:], in_=hid[:])

from contextlib import ExitStack

import concourse.mybir as mybir

K, T, J, R, C, O, N = 512, 1024, 256, 512, 512, 128, 256
FLOPS = 2 * (2 * K * R * J + R * N * O + K * N * O)

F32 = mybir.dt.float32
BF16 = mybir.dt.bfloat16
I32 = mybir.dt.int32
U32 = mybir.dt.uint32
U16 = mybir.dt.uint16
U8 = mybir.dt.uint8
E4M3 = mybir.dt.float8_e4m3fn_x4
E5M2 = mybir.dt.float8_e5m2_x4
E2M1 = mybir.dt.float4_e2m1fn_x4
COPY = mybir.ActivationFunctionType.Copy
MAX = mybir.AluOpType.max

P = 128
PACK = 4


def load_words(queue, tile, words):
    queue.dma_start(out=tile[:].bitcast(I32), in_=words.bitcast(I32))


def load_scale_rows(queue, tile, scales, q):
    queue.dma_start(out=tile[32 * q : 32 * q + 4, :].bitcast(I32), in_=scales[0, 4 * q : 4 * q + 4, :].bitcast(I32))


def load_scale_quadrant(queue, tile, scales, q):
    rows = scales[0, 4 * q : 4 * q + 4, :].bitcast(I32)
    queue.dma_start(out=tile[32 * q : 32 * q + 32, :].bitcast(I32),
                    in_=rows.unsqueeze(0).broadcast_to([8, 4, rows.shape[1]]))


def tile_list_postbox_twow_further_plain_kernel(
    tc, xt_words, xt_scales, w_words, w_scales, w2_words, w2_scales, wb_words, wb_scales,
    ws_words, ws_scales, offs, offs2, offs3, offs4, offs5, out,
):
    nc = tc.nc
    with ExitStack() as ctx:
        pool = ctx.enter_context(tc.tile_pool(name="held", bufs=1))
        psum = ctx.enter_context(tc.psum_pool(name="psum", bufs=1))

        def sbuf(name, shape, dtype):
            return pool.tile(shape, dtype, name=name, align_bytes=64)

        def flat(words):
            return words[0].rearrange("p n t -> p (n t)")

        def load_list(name, src):
            tile = pool.tile(list(src.shape), U16, name=name)
            nc.sync.dma_start(tile[:], src)
            return tile

        xt_w = sbuf("xt_w", [P, T], U32)
        xt_s = sbuf("xt_s", [P, T], U8)
        w_raw = sbuf("w_raw", [P, R], U16)
        w_sraw = sbuf("w_sraw", [P, R], U8)
        w2_raw = sbuf("w2_raw", [P, R], U32)
        w2_sraw = sbuf("w2_sraw", [P, R], U8)
        wb_w = sbuf("wb_w", [P, N], U32)
        wb_s = sbuf("wb_s", [P, N], U8)
        ws_w = sbuf("ws_w", [P, N], U32)
        ws_s = sbuf("ws_s", [P, N], U8)

        nc.vector.memset(w_sraw[:].bitcast(I32), 0)
        for plane in (w2_sraw, ws_s, wb_s):
            nc.gpsimd.memset(plane[:].bitcast(I32), 0)

        idx = load_list("idx", offs)
        for q in range(4):
            load_scale_quadrant(nc.sync, xt_s, xt_scales, q)
        load_words(nc.sync, xt_w, flat(xt_words))
        load_words(nc.sync, w_raw, w_words[0])
        for q in range(4):
            load_scale_rows(nc.sync, w_sraw, w_scales, q)
        idx5 = load_list("idx5", offs5)
        idx2 = load_list("idx2", offs2)
        load_words(nc.sync, w2_raw, flat(w2_words))
        for q in range(4):
            load_scale_rows(nc.sync, w2_sraw, w2_scales, q)
        idx3 = load_list("idx3", offs3)
        idx4 = load_list("idx4", offs4)
        load_words(nc.sync, ws_w, flat(ws_words))
        for q in range(4):
            load_scale_rows(nc.sync, ws_s, ws_scales, q)
        load_words(nc.sync, wb_w, flat(wb_words))
        for q in range(4):
            load_scale_rows(nc.sync, wb_s, wb_scales, q)

        boards = [sbuf("board%d" % t, [P, C], F32) for t in range(PACK)]
        for t in range(PACK):
            nc.vector.memset(boards[t][:], 0.0)

        w_w = sbuf("w_w", [P, R], U16)
        w_s = sbuf("w_s", [P, R], U8)
        w2_w = sbuf("w2_w", [P, R], U32)
        w2_s = sbuf("w2_s", [P, R], U8)
        nc.gpsimd.tensor_copy(
            out=w2_w[:].rearrange("p (t c i) -> p c t i", t=PACK, i=4),
            in_=w2_raw[:].rearrange("p (c i t) -> p c t i", t=PACK, i=4))
        nc.gpsimd.tensor_copy(
            out=w2_s[:].rearrange("p (t m) -> p t m", t=PACK), in_=w2_sraw[:].rearrange("p (m t) -> p t m", t=PACK))

        xg_w = sbuf("xg_w", [P, J], U32)
        xg_s = sbuf("xg_s", [P, J], U8)
        x5_w = sbuf("x5_w", [P, O], U32)
        x5_s = sbuf("x5_s", [P, O], U8)
        nc.vector.tensor_copy(out=xg_s[:], in_=xt_s[:].indirect(idx[:]))
        nc.scalar.copy(
            out=w_w[:].rearrange("p (t m) -> p t m", t=PACK), in_=w_raw[:].rearrange("p (m t) -> p t m", t=PACK))
        nc.vector.tensor_copy(out=xg_w[:], in_=xt_w[:].indirect(idx[:]))
        for t in range(PACK):
            nc.vector.tensor_copy(
                out=w_s[:, t * P : (t + 1) * P], in_=w_sraw[:].rearrange("p (m t) -> p t m", t=PACK)[:, t, :])
        nc.vector.tensor_copy(out=x5_s[:], in_=xt_s[:].indirect(idx5[:]))
        nc.vector.tensor_copy(out=x5_w[:], in_=xt_w[:].indirect(idx5[:]))

        def first_stage(acc, words, scales, fmt, t):
            cols = slice(t * P, (t + 1) * P)
            nc.tensor.matmul_mx(out=acc, lhsT=words[:, cols].bitcast(fmt), lhsT_scale=scales[:, cols],
                                rhs=xg_w[:].bitcast(E4M3), rhs_scale=xg_s[:], start=True, stop=True)

        a_ps = [psum.tile([P, J], F32, name="a_ps%d" % t) for t in range(PACK)]
        b_ps = [psum.tile([P, 2, J], F32, name="b_ps%d" % u) for u in range(2)]
        y_ps = [psum.tile([P, O], F32, name="y_ps%d" % h) for h in range(2)]
        for t in range(PACK):
            first_stage(a_ps[t][:], w_w, w_s, E2M1, t)
        for t in range(PACK):
            first_stage(b_ps[t // 2][:, t % 2, :], w2_w, w2_s, E5M2, t)
        for h in range(2):
            cols = slice(h * P, (h + 1) * P)
            nc.tensor.matmul_mx(out=y_ps[h][:], lhsT=ws_w[:, cols].bitcast(E5M2), lhsT_scale=ws_s[:, cols],
                                rhs=x5_w[:].bitcast(E4M3), rhs_scale=x5_s[:], start=True, stop=False)

        def move(on_scalar, dst, src):
            if on_scalar:
                nc.scalar.activation(out=dst, in_=src, func=COPY)
            else:
                nc.vector.tensor_copy(out=dst, in_=src)

        a_sb = [sbuf("a_sb%d" % t, [P, J], F32) for t in range(PACK)]
        b_sb = [sbuf("b_sb%d" % u, [P, 2 * J], F32) for u in range(2)]
        from_board = sbuf("from_board", [P, PACK, O], F32)
        from_b = sbuf("from_b", [P, PACK, O], F32)
        for t in range(PACK):
            move(t % 2 == 0, a_sb[t][:], a_ps[t][:])
        for t in range(PACK):
            move(t % 2 == 0, boards[t][:].indirect(idx2[:]), a_sb[t][:])
        for u in range(2):
            move(u == 0, b_sb[u][:], b_ps[u][:].rearrange("p t j -> p (t j)"))
        for t in range(PACK):
            move(t % 2 == 0, from_board[:, t, :], boards[t][:].indirect(idx3[:]))
        for t in range(PACK):
            window = b_sb[t // 2][:, (t % 2) * J : (t % 2 + 1) * J]
            move(t != 1, from_b[:, t, :], window.indirect(idx4[:]))

        hid = sbuf("hid", [P, O * PACK], BF16)
        for u in range(2):
            pair = slice(2 * u, 2 * u + 2)
            nc.vector.tensor_tensor(
                out=hid[:].rearrange("p (c i t) -> p c t i", t=PACK, i=4)[:, :, pair, :],
                in0=from_board[:, pair, :].rearrange("p t (c i) -> p c t i", i=4),
                in1=from_b[:, pair, :].rearrange("p t (c i) -> p c t i", i=4), op=MAX)
        hid_w = sbuf("hid_w", [P, O], U32)
        hid_s = sbuf("hid_s", [P, O], U8)
        nc.vector.quantize_mx(out=hid_w[:].bitcast(E4M3), scales=hid_s[:], in_=hid[:])

        for h in range(2):
            cols = slice(h * P, (h + 1) * P)
            nc.tensor.matmul_mx(out=y_ps[h][:], lhsT=wb_w[:, cols].bitcast(E5M2), lhsT_scale=wb_s[:, cols],
                                rhs=hid_w[:].bitcast(E4M3), rhs_scale=hid_s[:], start=False, stop=True)
            y_sb = sbuf("y_sb%d" % h, [P, O], F32)
            move(h == 1, y_sb[:], y_ps[h][:])
            (nc.scalar if h == 1 else nc.sync).dma_start(out=out[cols, :], in_=y_sb[:])
